import numpy as np
import ml_dtypes


def mxq(x, axis, fmt="e4m3"):
    dtype, down = {"e4m3": (ml_dtypes.float8_e4m3fn, 7), "e5m2": (ml_dtypes.float8_e5m2, 14)}[fmt]
    v = np.moveaxis(np.asarray(x, np.float32).astype(ml_dtypes.bfloat16).astype(np.float64), axis, -1)
    blocks = v.reshape(v.shape[:-1] + (-1, 32))
    amax = np.abs(blocks).max(-1, keepdims=True)
    byte = np.maximum(np.where(amax > 0, np.frexp(amax)[1] - 1 + 127, 0) - down, 1)
    scale = np.exp2(byte - 127.0)
    codes = (blocks / scale).astype(np.float32).astype(dtype).astype(np.float64)
    return np.moveaxis((codes * scale).reshape(v.shape), -1, axis)


WIDE = False


def mx_kscale(k):
    if not WIDE:
        return np.ones(k)
    levels = np.array([10, -10, 5, -5, 0])
    if k % 512:
        return np.exp2(np.random.permutation(np.resize(levels, k // 32))).repeat(32)
    a = np.empty((k // 512, 16))
    for p in range(k // 512):
        a[p, :8] = np.random.permutation(np.resize(levels, 8))
        for g in range(8):
            far = levels[np.abs(levels - a[p, g]) >= 10]
            a[p, g + 8] = far[np.random.randint(len(far))]
    return np.exp2(a.ravel()).repeat(32)


def f64(x):
    return np.asarray(x).astype(np.float64)


E2M1 = np.array([0.0, 0.5, 1.0, 1.5, 2.0, 3.0, 4.0, 6.0, -0.0, -0.5, -1.0, -1.5, -2.0, -3.0, -4.0, -6.0])


def pack_weight(w, fmt):
    k, n = w.shape
    w = f64(np.asarray(w, np.float32).astype(ml_dtypes.bfloat16)).reshape(k // 32, 32, n)
    amax = np.abs(w).max(1)
    if fmt == "e4m3":
        byte = np.frexp(amax)[1] - 1 + 127 - 7
    else:
        mant, ex = np.frexp(amax / 6.0)
        byte = np.where(mant > 0.5, ex, ex - 1) + 127
    byte = np.clip(np.where(amax > 0, byte, 1), 1, 254)
    scaled = (w * np.exp2(127.0 - byte)[:, None, :]).reshape(k, n).astype(np.float32)
    by_word = np.ascontiguousarray(scaled.reshape(k // 512, 128, 4, n).transpose(0, 1, 3, 2))
    if fmt == "e4m3":
        words = by_word.astype(ml_dtypes.float8_e4m3fn).view(np.uint8)
    else:
        c = by_word.astype(ml_dtypes.float4_e2m1fn).view(np.uint8) & 0xF
        words = (c[..., 0::2] | (c[..., 1::2] << 4)).reshape(k // 512, 128, 2 * n)
    return np.ascontiguousarray(words), np.ascontiguousarray(byte.astype(np.uint8).reshape(k // 512, 16, n))


def unpack_weight(words, scales, fmt):
    g, _, n = scales.shape
    words = np.ascontiguousarray(words).reshape(g, 128, n, -1)
    if fmt == "e4m3":
        vals = words.view(ml_dtypes.float8_e4m3fn).astype(np.float64)
    else:
        nib = np.empty((g, 128, n, 4), np.uint8)
        nib[..., 0::2] = words & 0xF
        nib[..., 1::2] = words >> 4
        vals = E2M1[nib]
    vals = vals * np.repeat(np.exp2(scales.astype(np.float64) - 127.0), 8, axis=1)[..., None]
    return vals.transpose(0, 1, 3, 2).reshape(g * 512, n)


def bf(x):
    return np.asarray(x, np.float32).astype(ml_dtypes.bfloat16)


def planes(Y):
    r, m = Y.shape
    b = f64(bf(Y)).reshape(r // 32, 32, m)
    amax = np.abs(b).max(1)
    byte = np.clip(np.where(amax > 0, np.frexp(amax)[1] - 1 + 127 - 7, 1), 1, 254)
    codes = (b * np.exp2(127.0 - byte)[:, None, :]).reshape(r, m).astype(np.float32).astype(ml_dtypes.float8_e4m3fn).view(np.uint8)
    words = codes.reshape(r // 512, 128, 4, m).transpose(0, 1, 3, 2)
    return np.ascontiguousarray(words), np.ascontiguousarray(byte.astype(np.uint8).reshape(r // 512, 16, m))


K, T, R, N, B = 1024, 512, 512, 512, 128


def setup_inputs():
    n = np.random.standard_normal
    fk = mx_kscale(K)
    fr = mx_kscale(R)
    xtp = pack_weight(n((K, T)) / fk[:, None], "e2m1")
    wap = pack_weight(n((K, R)) * 1 / np.sqrt(K) * fk[:, None] * fr, "e4m3")
    wbp = pack_weight(n((R, N)) * 1 / np.sqrt(R) / fr[:, None], "e2m1")
    wyp = pack_weight(n((K, N)) * 1 / np.sqrt(K) * fk[:, None], "e4m3")
    return {
        "xt_words": xtp[0],
        "xt_scales": xtp[1],
        "wa_words": wap[0],
        "wa_scales": wap[1],
        "wb_words": wbp[0],
        "wb_scales": wbp[1],
        "wy_words": wyp[0],
        "wy_scales": wyp[1],
    }


def reference(xt_words, xt_scales, wa_words, wa_scales, wb_words, wb_scales, wy_words, wy_scales):
    xtu = unpack_weight(xt_words, xt_scales, "e2m1")
    wau = unpack_weight(wa_words, wa_scales, "e4m3")
    wbu = unpack_weight(wb_words, wb_scales, "e2m1")
    wyu = unpack_weight(wy_words, wy_scales, "e4m3")
    a = wau.T @ xtu
    m = a.reshape(R, B, T // B).mean(axis=2)
    mr = np.repeat(m, T // B, axis=1)
    hid = np.maximum(a - mr, 0.0)
    hidq = mxq(hid, 0, "e4m3")
    y = wbu.T @ hidq + wyu.T @ xtu
    words, scales = planes(y)
    return y, words, scales

@@ -1,0 +1,259 @@
+from contextlib import ExitStack
+
+import concourse.mybir as mybir
+
+K, T, R, N = 1024, 512, 512, 512
+FLOPS = 2 * K * R * T + 2 * R * N * T + 2 * K * N * T
+
+F32 = mybir.dt.float32
+BF16 = mybir.dt.bfloat16
+I32 = mybir.dt.int32
+U32 = mybir.dt.uint32
+U8 = mybir.dt.uint8
+FP8X4 = mybir.dt.float8_e4m3fn_x4
+FP4X4 = mybir.dt.float4_e2m1fn_x4
+ALU = mybir.AluOpType
+ACT = mybir.ActivationFunctionType
+
+P = 128
+PACK = 4
+PASSES = K // (P * PACK)
+CHUNK = 128
+CHUNKS = T // CHUNK
+GROUP = 4
+
+
+def tile_mix_hidden_less_group_and_skip_pl_kernel(
+    tc, xt_words, xt_scales, wa_words, wa_scales, wb_words, wb_scales, wy_words, wy_scales, out_0, out_1, out_2
+):
+    nc = tc.nc
+    with ExitStack() as ctx:
+        sb = ctx.enter_context(tc.tile_pool(name="sb", bufs=1))
+        ps = ctx.enter_context(tc.psum_pool(name="ps", bufs=1))
+        ctx.enter_context(tc.manual_schedule())
+
+        def tiles(pool, name, count, shape, dtype):
+            if pool is ps:
+                return [pool.tile(shape, dtype, name="%s%d" % (name, c)) for c in range(count)]
+            return [pool.tile(shape, dtype, name="%s%d" % (name, c), align_bytes=64) for c in range(count)]
+
+        x_codes = sb.tile([P, PASSES, 2 * T], U8, align_bytes=64)
+        x_plane = sb.tile([P, PASSES, T], U8, align_bytes=64)
+        wa_raw = sb.tile([P, PASSES, R], U32, align_bytes=64)
+        wa_codes = tiles(sb, "wa_codes", PASSES, [P, R], U32)
+        wa_rows = sb.tile([P, PASSES, R], U8, align_bytes=64)
+        wa_plane = tiles(sb, "wa_plane", PASSES, [P, R], U8)
+        wy_raw = sb.tile([P, PASSES, N], U32, align_bytes=64)
+        wy_codes = tiles(sb, "wy_codes", PASSES, [P, N], U32)
+        wy_rows = sb.tile([P, PASSES, N], U8, align_bytes=64)
+        wy_plane = tiles(sb, "wy_plane", PASSES, [P, N], U8)
+        wb_raw = sb.tile([P, 2 * N], U8, align_bytes=64)
+        wb_codes = sb.tile([P, 2 * N], U8, align_bytes=64)
+        wb_rows = sb.tile([P, 1, N], U8, align_bytes=64)
+        wb_plane = sb.tile([P, N], U8, align_bytes=64)
+
+        a_bank = tiles(ps, "a_bank", CHUNKS, [P, PACK, CHUNK], F32)
+        y_bank = tiles(ps, "y_bank", CHUNKS, [P, PACK, CHUNK], F32)
+        sums = tiles(sb, "sums", CHUNKS, [P, PACK, CHUNK // GROUP], F32)
+        means = tiles(sb, "means", CHUNKS, [P, CHUNK // GROUP, PACK], F32)
+        diff = tiles(sb, "diff", CHUNKS, [P, CHUNK * PACK], BF16)
+        hid = tiles(sb, "hid", CHUNKS, [P, CHUNK * PACK], BF16)
+        hid_codes = tiles(sb, "hid_codes", CHUNKS, [P, CHUNK], U32)
+        hid_plane = tiles(sb, "hid_plane", CHUNKS, [P, CHUNK], U8)
+        y_f32 = tiles(sb, "y_f32", CHUNKS, [P, PACK, CHUNK], F32)
+        y_bf16 = tiles(sb, "y_bf16", CHUNKS, [P, CHUNK * PACK], BF16)
+        y_codes = sb.tile([P, T], U32, align_bytes=64)
+        y_plane = sb.tile([P, T], U8, align_bytes=64)
+
+        def zero(engine, rows):
+            engine.memset(rows[:].rearrange("p z c -> p (z c)").bitcast(I32), 0)
+
+        def load_rows(queue, rows, scales, r):
+            src = scales.rearrange("z (q r) c -> r q z c", r=4)[r]
+            queue.dma_start(out=rows[r:P:32, :, :].bitcast(I32), in_=src.bitcast(I32))
+
+        def load_words(raw, words):
+            nc.sync.dma_start(out=raw[:].bitcast(I32), in_=words.rearrange("z p n t -> p z (n t)").bitcast(I32))
+
+        def deal_words(codes, raw):
+            nc.vector.tensor_copy(
+                out=codes[:].bitcast(I32).rearrange("p (j b m) -> p b j m", j=PACK, m=4),
+                in_=raw.bitcast(I32).rearrange("p (b m j) -> p b j m", j=PACK, m=4),
+            )
+
+        def deal_plane(engine, plane, rows):
+            engine.tensor_copy(
+                out=plane.rearrange("p (j m) -> p j m", j=PACK), in_=rows.rearrange("p (m j) -> p j m", j=PACK)
+            )
+
+        def x_product(bank, codes, plane, c, z, start, stop):
+            for j in range(PACK):
+                nc.tensor.matmul_mx(
+                    out=bank[:, j, :],
+                    lhsT=codes[z][:, P * j : P * (j + 1)].bitcast(FP8X4),
+                    lhsT_scale=plane[z][:, P * j : P * (j + 1)],
+                    rhs=x_codes[:, z, 2 * CHUNK * c : 2 * CHUNK * (c + 1)].bitcast(FP4X4),
+                    rhs_scale=x_plane[:, z, CHUNK * c : CHUNK * (c + 1)],
+                    start=(start and j == 0),
+                    stop=(stop and j == PACK - 1),
+                )
+
+        def first_layer(c):
+            for z in range(PASSES):
+                x_product(a_bank[c], wa_codes, wa_plane, c, z, z == 0, z == PASSES - 1)
+
+        def skip(c):
+            for z in range(PASSES):
+                x_product(y_bank[c], wy_codes, wy_plane, c, z, z == 0, False)
+
+        def second_layer(c):
+            for i in range(PACK):
+                nc.tensor.matmul_mx(
+                    out=y_bank[c][:, i, :],
+                    lhsT=wb_codes[:, 2 * P * i : 2 * P * (i + 1)].bitcast(FP4X4),
+                    lhsT_scale=wb_plane[:, P * i : P * (i + 1)],
+                    rhs=hid_codes[c][:].bitcast(FP8X4),
+                    rhs_scale=hid_plane[c][:],
+                    start=False,
+                    stop=(i == PACK - 1),
+                )
+
+        def group_sum(c):
+            nc.vector.tensor_reduce(
+                out=sums[c][:].rearrange("p j b -> p (j b)"),
+                in_=a_bank[c][:].rearrange("p j (b g) -> p (j b) g", g=GROUP),
+                axis=mybir.AxisListType.X,
+                op=ALU.add,
+            )
+
+        def group_mean(c):
+            nc.scalar.activation(
+                out=means[c][:], in_=sums[c][:].rearrange("p j b -> p b j"), func=ACT.Copy, scale=1.0 / GROUP
+            )
+
+        def subtract(c):
+            nc.vector.tensor_tensor(
+                out=diff[c][:].rearrange("p (b g j) -> p b g j", g=GROUP, j=PACK),
+                in0=a_bank[c][:].rearrange("p j (b g) -> p b g j", g=GROUP),
+                in1=means[c][:].unsqueeze(2).to_broadcast([P, CHUNK // GROUP, GROUP, PACK]),
+                op=ALU.subtract,
+            )
+
+        def relu_scalar(c):
+            nc.scalar.activation(out=hid[c][:], in_=diff[c][:], func=ACT.Relu)
+
+        def relu_vector(c):
+            nc.vector.tensor_scalar_max(out=hid[c][:], in0=diff[c][:], scalar1=0.0)
+
+        def quantize_hid(c):
+            nc.vector.quantize_mx(out=hid_codes[c][:].bitcast(FP8X4), scales=hid_plane[c][:], in_=hid[c][:])
+
+        def round_y(c):
+            nc.scalar.copy(
+                out=y_bf16[c][:].rearrange("p (t i) -> p t i", i=PACK), in_=y_bank[c][:].rearrange("p i t -> p t i")
+            )
+
+        def round_y_vector(c):
+            nc.vector.tensor_copy(
+                out=y_bf16[c][:].rearrange("p (b t i) -> p b i t", i=PACK, t=4),
+                in_=y_f32[c][:].rearrange("p i (b t) -> p b i t", t=4),
+            )
+
+        def deal_wb(engine):
+            engine.tensor_copy(
+                out=wb_codes[:].rearrange("p (i m h) -> p i m h", i=PACK, h=2),
+                in_=wb_raw[:].rearrange("p (m i h) -> p i m h", i=PACK, h=2),
+            )
+
+        def store_y(c):
+            nc.scalar.copy(out=y_f32[c][:], in_=y_bank[c][:])
+            nc.sync.dma_start(
+                out=out_0.rearrange("(p i) t -> p i t", i=PACK)[:, :, CHUNK * c : CHUNK * (c + 1)], in_=y_f32[c][:]
+            )
+
+        def quantize_y(c):
+            cols = slice(CHUNK * c, CHUNK * (c + 1))
+            nc.vector.quantize_mx(out=y_codes[:, cols].bitcast(FP8X4), scales=y_plane[:, cols], in_=y_bf16[c][:])
+            if c >= CHUNKS - 2:
+                cols = cols if c == CHUNKS - 1 else slice(0, CHUNK * (c + 1))
+                dst = out_1[0].rearrange("p n t -> p (n t)").bitcast(I32)
+                nc.sync.dma_start(out=dst[:, cols], in_=y_codes[:, cols].bitcast(I32))
+
+        zero(nc.vector, wa_rows)
+        zero(nc.gpsimd, x_plane)
+        zero(nc.vector, wy_rows)
+        zero(nc.vector, wb_rows)
+        for r in range(4):
+            load_rows(nc.scalar, wa_rows, wa_scales, r)
+        for r in range(2):
+            load_rows(nc.scalar, x_plane, xt_scales, r)
+        for r in range(2, 4):
+            load_rows(nc.gpsimd, x_plane, xt_scales, r)
+        load_words(wa_raw, wa_words)
+        nc.sync.dma_start(out=x_codes[:].bitcast(I32), in_=xt_words.rearrange("z p c -> p z c").bitcast(I32))
+        load_words(wy_raw, wy_words)
+        for r in range(4):
+            load_rows(nc.sync, wy_rows, wy_scales, r)
+        nc.sync.dma_start(out=wb_raw[:].bitcast(I32), in_=wb_words[0].bitcast(I32))
+        for r in range(4):
+            load_rows(nc.sync, wb_rows, wb_scales, r)
+
+        deal_plane(nc.vector, wa_plane[0][:], wa_rows[:, 0, :])
+        deal_plane(nc.vector, wa_plane[1][:], wa_rows[:, 1, :])
+        deal_words(wa_codes[0], wa_raw[:, 0, :])
+        deal_words(wa_codes[1], wa_raw[:, 1, :])
+        first_layer(0)
+        first_layer(1)
+        first_layer(2)
+        first_layer(3)
+        deal_words(wy_codes[0], wy_raw[:, 0, :])
+        deal_words(wy_codes[1], wy_raw[:, 1, :])
+        group_sum(0)
+        group_mean(0)
+        deal_plane(nc.vector, wy_plane[0][:], wy_rows[:, 0, :])
+        subtract(0)
+        relu_scalar(0)
+        group_sum(1)
+        group_mean(1)
+        deal_plane(nc.vector, wy_plane[1][:], wy_rows[:, 1, :])
+        skip(0)
+        skip(1)
+        subtract(1)
+        relu_scalar(1)
+        quantize_hid(0)
+        group_sum(2)
+        group_mean(2)
+        deal_wb(nc.vector)
+        deal_plane(nc.vector, wb_plane[:], wb_rows[:, 0, :])
+        second_layer(0)
+        skip(2)
+        subtract(2)
+        relu_scalar(2)
+        quantize_hid(1)
+        second_layer(1)
+        skip(3)
+        group_sum(3)
+        group_mean(3)
+        store_y(0)
+        quantize_hid(2)
+        second_layer(2)
+        subtract(3)
+        store_y(1)
+        relu_vector(3)
+        round_y_vector(0)
+        quantize_hid(3)
+        second_layer(3)
+        store_y(2)
+        round_y_vector(1)
+        quantize_y(0)
+        round_y_vector(2)
+        quantize_y(1)
+        quantize_y(2)
+        store_y(3)
+        round_y_vector(3)
+        quantize_y(3)
+        for q in range(4):
+            queue = nc.sync if q < 2 else nc.scalar
+            queue.dma_start(
+                out=out_2[0, 4 * q : 4 * q + 4, :].bitcast(I32), in_=y_plane[32 * q : 32 * q + 4, :].bitcast(I32)
+            )

@@ -180,17 +180,15 @@ def tile_mix_hidden_less_group_and_skip_pl_kernel(
                 nc.sync.dma_start(out=dst[:, cols], in_=y_codes[:, cols].bitcast(I32))
 
         zero(nc.vector, wa_rows)
-        zero(nc.gpsimd, x_plane)
+        zero(nc.vector, x_plane)
         zero(nc.vector, wy_rows)
         zero(nc.vector, wb_rows)
         for r in range(4):
-            load_rows(nc.scalar, wa_rows, wa_scales, r)
-        for r in range(2):
-            load_rows(nc.scalar, x_plane, xt_scales, r)
-        for r in range(2, 4):
-            load_rows(nc.gpsimd, x_plane, xt_scales, r)
+            load_rows(nc.sync if r < 2 else nc.scalar, wa_rows, wa_scales, r)
         load_words(wa_raw, wa_words)
         nc.sync.dma_start(out=x_codes[:].bitcast(I32), in_=xt_words.rearrange("z p c -> p z c").bitcast(I32))
+        for r in range(4):
+            load_rows(nc.scalar, x_plane, xt_scales, r)
         load_words(wy_raw, wy_words)
         for r in range(4):
             load_rows(nc.sync, wy_rows, wy_scales, r)
@@ -206,38 +204,38 @@ def tile_mix_hidden_less_group_and_skip_pl_kernel(
         first_layer(1)
         first_layer(2)
         first_layer(3)
+        deal_plane(nc.gpsimd, wy_plane[0][:], wy_rows[:, 0, :])
+        deal_plane(nc.gpsimd, wy_plane[1][:], wy_rows[:, 1, :])
+        deal_wb(nc.gpsimd)
+        deal_plane(nc.gpsimd, wb_plane[:], wb_rows[:, 0, :])
         deal_words(wy_codes[0], wy_raw[:, 0, :])
-        deal_words(wy_codes[1], wy_raw[:, 1, :])
         group_sum(0)
         group_mean(0)
-        deal_plane(nc.vector, wy_plane[0][:], wy_rows[:, 0, :])
-        subtract(0)
-        relu_scalar(0)
+        deal_words(wy_codes[1], wy_raw[:, 1, :])
         group_sum(1)
         group_mean(1)
-        deal_plane(nc.vector, wy_plane[1][:], wy_rows[:, 1, :])
+        subtract(0)
+        relu_scalar(0)
+        group_sum(2)
+        group_mean(2)
         skip(0)
         skip(1)
+        skip(2)
         subtract(1)
         relu_scalar(1)
         quantize_hid(0)
-        group_sum(2)
-        group_mean(2)
-        deal_wb(nc.vector)
-        deal_plane(nc.vector, wb_plane[:], wb_rows[:, 0, :])
         second_layer(0)
-        skip(2)
-        subtract(2)
-        relu_scalar(2)
-        quantize_hid(1)
-        second_layer(1)
-        skip(3)
         group_sum(3)
         group_mean(3)
+        skip(3)
+        subtract(2)
+        quantize_hid(1)
+        second_layer(1)
         store_y(0)
+        relu_vector(2)
+        subtract(3)
         quantize_hid(2)
         second_layer(2)
-        subtract(3)
         store_y(1)
         relu_vector(3)
         round_y_vector(0)
@@ -248,8 +246,8 @@ def tile_mix_hidden_less_group_and_skip_pl_kernel(
         quantize_y(0)
         round_y_vector(2)
         quantize_y(1)
-        quantize_y(2)
         store_y(3)
+        quantize_y(2)
         round_y_vector(3)
         quantize_y(3)
         for q in range(4):

@@ -21,6 +21,10 @@ PASSES = K // (P * PACK)
 CHUNK = 128
 CHUNKS = T // CHUNK
 GROUP = 4
+QUADRANT = 32
+ROWS = 4
+LINE = 4
+SCALAR_RELU_CHUNKS = 2
 
 
 def tile_mix_hidden_less_group_and_skip_pl_kernel(
@@ -32,106 +36,83 @@ def tile_mix_hidden_less_group_and_skip_pl_kernel(
         ps = ctx.enter_context(tc.psum_pool(name="ps", bufs=1))
         ctx.enter_context(tc.manual_schedule())
 
-        def tiles(pool, name, count, shape, dtype):
-            if pool is ps:
-                return [pool.tile(shape, dtype, name="%s%d" % (name, c)) for c in range(count)]
-            return [pool.tile(shape, dtype, name="%s%d" % (name, c), align_bytes=64) for c in range(count)]
+        def sbuf_tiles(name, count, shape, dtype):
+            return [sb.tile(shape, dtype, name="%s%d" % (name, c), align_bytes=64) for c in range(count)]
+
+        def psum_banks(name):
+            return [ps.tile([P, PACK, CHUNK], F32, name="%s%d" % (name, c)) for c in range(CHUNKS)]
 
         x_codes = sb.tile([P, PASSES, 2 * T], U8, align_bytes=64)
         x_plane = sb.tile([P, PASSES, T], U8, align_bytes=64)
         wa_raw = sb.tile([P, PASSES, R], U32, align_bytes=64)
-        wa_codes = tiles(sb, "wa_codes", PASSES, [P, R], U32)
+        wa_codes = sbuf_tiles("wa_codes", PASSES, [P, R], U32)
         wa_rows = sb.tile([P, PASSES, R], U8, align_bytes=64)
-        wa_plane = tiles(sb, "wa_plane", PASSES, [P, R], U8)
+        wa_plane = sbuf_tiles("wa_plane", PASSES, [P, R], U8)
         wy_raw = sb.tile([P, PASSES, N], U32, align_bytes=64)
-        wy_codes = tiles(sb, "wy_codes", PASSES, [P, N], U32)
+        wy_codes = sb.tile([P, PASSES, N], U32, align_bytes=64)
         wy_rows = sb.tile([P, PASSES, N], U8, align_bytes=64)
-        wy_plane = tiles(sb, "wy_plane", PASSES, [P, N], U8)
+        wy_plane = sb.tile([P, PASSES, N], U8, align_bytes=64)
         wb_raw = sb.tile([P, 2 * N], U8, align_bytes=64)
         wb_codes = sb.tile([P, 2 * N], U8, align_bytes=64)
         wb_rows = sb.tile([P, 1, N], U8, align_bytes=64)
         wb_plane = sb.tile([P, N], U8, align_bytes=64)
 
-        a_bank = tiles(ps, "a_bank", CHUNKS, [P, PACK, CHUNK], F32)
-        y_bank = tiles(ps, "y_bank", CHUNKS, [P, PACK, CHUNK], F32)
-        sums = tiles(sb, "sums", CHUNKS, [P, PACK, CHUNK // GROUP], F32)
-        means = tiles(sb, "means", CHUNKS, [P, CHUNK // GROUP, PACK], F32)
-        diff = tiles(sb, "diff", CHUNKS, [P, CHUNK * PACK], BF16)
-        hid = tiles(sb, "hid", CHUNKS, [P, CHUNK * PACK], BF16)
-        hid_codes = tiles(sb, "hid_codes", CHUNKS, [P, CHUNK], U32)
-        hid_plane = tiles(sb, "hid_plane", CHUNKS, [P, CHUNK], U8)
-        y_f32 = tiles(sb, "y_f32", CHUNKS, [P, PACK, CHUNK], F32)
-        y_bf16 = tiles(sb, "y_bf16", CHUNKS, [P, CHUNK * PACK], BF16)
+        a_bank = psum_banks("a_bank")
+        y_bank = psum_banks("y_bank")
+        sums = sbuf_tiles("sums", CHUNKS, [P, PACK, CHUNK // GROUP], F32)
+        means = sbuf_tiles("means", CHUNKS, [P, CHUNK // GROUP, PACK], F32)
+        diff = sbuf_tiles("diff", CHUNKS, [P, CHUNK * PACK], BF16)
+        hid = sbuf_tiles("hid", CHUNKS, [P, CHUNK * PACK], BF16)
+        hid_codes = sbuf_tiles("hid_codes", CHUNKS, [P, CHUNK], U32)
+        hid_plane = sbuf_tiles("hid_plane", CHUNKS, [P, CHUNK], U8)
+        y_f32 = sbuf_tiles("y_f32", CHUNKS, [P, PACK, CHUNK], F32)
+        y_bf16 = sbuf_tiles("y_bf16", CHUNKS, [P, CHUNK * PACK], BF16)
         y_codes = sb.tile([P, T], U32, align_bytes=64)
         y_plane = sb.tile([P, T], U8, align_bytes=64)
+
+        def chunk_cols(c):
+            return slice(CHUNK * c, CHUNK * (c + 1))
 
         def zero(engine, rows):
             engine.memset(rows[:].rearrange("p z c -> p (z c)").bitcast(I32), 0)
 
         def load_rows(queue, rows, scales, r):
-            src = scales.rearrange("z (q r) c -> r q z c", r=4)[r]
-            queue.dma_start(out=rows[r:P:32, :, :].bitcast(I32), in_=src.bitcast(I32))
+            src = scales.rearrange("z (q r) c -> r q z c", r=ROWS)[r]
+            queue.dma_start(out=rows[r:P:QUADRANT, :, :].bitcast(I32), in_=src.bitcast(I32))
 
         def load_words(raw, words):
             nc.sync.dma_start(out=raw[:].bitcast(I32), in_=words.rearrange("z p n t -> p z (n t)").bitcast(I32))
-
-        def deal_words(codes, raw):
-            nc.vector.tensor_copy(
-                out=codes[:].bitcast(I32).rearrange("p (j b m) -> p b j m", j=PACK, m=4),
-                in_=raw.bitcast(I32).rearrange("p (b m j) -> p b j m", j=PACK, m=4),
-            )
 
         def deal_plane(engine, plane, rows):
             engine.tensor_copy(
                 out=plane.rearrange("p (j m) -> p j m", j=PACK), in_=rows.rearrange("p (m j) -> p j m", j=PACK)
             )
 
-        def x_product(bank, codes, plane, c, z, start, stop):
-            for j in range(PACK):
-                nc.tensor.matmul_mx(
-                    out=bank[:, j, :],
-                    lhsT=codes[z][:, P * j : P * (j + 1)].bitcast(FP8X4),
-                    lhsT_scale=plane[z][:, P * j : P * (j + 1)],
-                    rhs=x_codes[:, z, 2 * CHUNK * c : 2 * CHUNK * (c + 1)].bitcast(FP4X4),
-                    rhs_scale=x_plane[:, z, CHUNK * c : CHUNK * (c + 1)],
-                    start=(start and j == 0),
-                    stop=(stop and j == PACK - 1),
-                )
-
-        def first_layer(c):
+        def x_product(bank, codes, planes, c, closes_group):
             for z in range(PASSES):
-                x_product(a_bank[c], wa_codes, wa_plane, c, z, z == 0, z == PASSES - 1)
+                for j in range(PACK):
+                    nc.tensor.matmul_mx(
+                        out=bank[:, j, :],
+                        lhsT=codes[z][:, P * j : P * (j + 1)].bitcast(FP8X4),
+                        lhsT_scale=planes[z][:, P * j : P * (j + 1)],
+                        rhs=x_codes[:, z, 2 * CHUNK * c : 2 * CHUNK * (c + 1)].bitcast(FP4X4),
+                        rhs_scale=x_plane[:, z, chunk_cols(c)],
+                        start=(z == 0 and j == 0),
+                        stop=(closes_group and z == PASSES - 1 and j == PACK - 1),
+                    )
 
-        def skip(c):
-            for z in range(PASSES):
-                x_product(y_bank[c], wy_codes, wy_plane, c, z, z == 0, False)
-
-        def second_layer(c):
-            for i in range(PACK):
-                nc.tensor.matmul_mx(
-                    out=y_bank[c][:, i, :],
-                    lhsT=wb_codes[:, 2 * P * i : 2 * P * (i + 1)].bitcast(FP4X4),
-                    lhsT_scale=wb_plane[:, P * i : P * (i + 1)],
-                    rhs=hid_codes[c][:].bitcast(FP8X4),
-                    rhs_scale=hid_plane[c][:],
-                    start=False,
-                    stop=(i == PACK - 1),
-                )
-
-        def group_sum(c):
+        def group_mean(c):
             nc.vector.tensor_reduce(
                 out=sums[c][:].rearrange("p j b -> p (j b)"),
                 in_=a_bank[c][:].rearrange("p j (b g) -> p (j b) g", g=GROUP),
                 axis=mybir.AxisListType.X,
                 op=ALU.add,
             )
-
-        def group_mean(c):
             nc.scalar.activation(
                 out=means[c][:], in_=sums[c][:].rearrange("p j b -> p b j"), func=ACT.Copy, scale=1.0 / GROUP
             )
 
-        def subtract(c):
+        def subtract_mean(c):
             nc.vector.tensor_tensor(
                 out=diff[c][:].rearrange("p (b g j) -> p b g j", g=GROUP, j=PACK),
                 in0=a_bank[c][:].rearrange("p j (b g) -> p b g j", g=GROUP),
@@ -139,119 +120,109 @@ def tile_mix_hidden_less_group_and_skip_pl_kernel(
                 op=ALU.subtract,
             )
 
-        def relu_scalar(c):
-            nc.scalar.activation(out=hid[c][:], in_=diff[c][:], func=ACT.Relu)
-
-        def relu_vector(c):
-            nc.vector.tensor_scalar_max(out=hid[c][:], in0=diff[c][:], scalar1=0.0)
-
-        def quantize_hid(c):
+        def second_layer(c):
             nc.vector.quantize_mx(out=hid_codes[c][:].bitcast(FP8X4), scales=hid_plane[c][:], in_=hid[c][:])
-
-        def round_y(c):
-            nc.scalar.copy(
-                out=y_bf16[c][:].rearrange("p (t i) -> p t i", i=PACK), in_=y_bank[c][:].rearrange("p i t -> p t i")
-            )
-
-        def round_y_vector(c):
-            nc.vector.tensor_copy(
-                out=y_bf16[c][:].rearrange("p (b t i) -> p b i t", i=PACK, t=4),
-                in_=y_f32[c][:].rearrange("p i (b t) -> p b i t", t=4),
-            )
-
-        def deal_wb(engine):
-            engine.tensor_copy(
-                out=wb_codes[:].rearrange("p (i m h) -> p i m h", i=PACK, h=2),
-                in_=wb_raw[:].rearrange("p (m i h) -> p i m h", i=PACK, h=2),
-            )
+            for j in range(PACK):
+                nc.tensor.matmul_mx(
+                    out=y_bank[c][:, j, :],
+                    lhsT=wb_codes[:, 2 * P * j : 2 * P * (j + 1)].bitcast(FP4X4),
+                    lhsT_scale=wb_plane[:, P * j : P * (j + 1)],
+                    rhs=hid_codes[c][:].bitcast(FP8X4),
+                    rhs_scale=hid_plane[c][:],
+                    start=False,
+                    stop=(j == PACK - 1),
+                )
 
         def store_y(c):
             nc.scalar.copy(out=y_f32[c][:], in_=y_bank[c][:])
-            nc.sync.dma_start(
-                out=out_0.rearrange("(p i) t -> p i t", i=PACK)[:, :, CHUNK * c : CHUNK * (c + 1)], in_=y_f32[c][:]
+            nc.sync.dma_start(out=out_0.rearrange("(p j) t -> p j t", j=PACK)[:, :, chunk_cols(c)], in_=y_f32[c][:])
+
+        def round_y(c):
+            nc.vector.tensor_copy(
+                out=y_bf16[c][:].rearrange("p (b t j) -> p b j t", j=PACK, t=LINE),
+                in_=y_f32[c][:].rearrange("p j (b t) -> p b j t", t=LINE),
             )
 
         def quantize_y(c):
-            cols = slice(CHUNK * c, CHUNK * (c + 1))
+            cols = chunk_cols(c)
             nc.vector.quantize_mx(out=y_codes[:, cols].bitcast(FP8X4), scales=y_plane[:, cols], in_=y_bf16[c][:])
-            if c >= CHUNKS - 2:
-                cols = cols if c == CHUNKS - 1 else slice(0, CHUNK * (c + 1))
-                dst = out_1[0].rearrange("p n t -> p (n t)").bitcast(I32)
-                nc.sync.dma_start(out=dst[:, cols], in_=y_codes[:, cols].bitcast(I32))
+
+        def store_y_codes(cols):
+            dst = out_1[0].rearrange("p n t -> p (n t)").bitcast(I32)
+            nc.sync.dma_start(out=dst[:, cols], in_=y_codes[:, cols].bitcast(I32))
 
         zero(nc.vector, wa_rows)
-        zero(nc.vector, x_plane)
+        zero(nc.gpsimd, x_plane)
         zero(nc.vector, wy_rows)
         zero(nc.vector, wb_rows)
-        for r in range(4):
-            load_rows(nc.sync if r < 2 else nc.scalar, wa_rows, wa_scales, r)
+        for r in range(ROWS):
+            load_rows(nc.sync if r < ROWS // 2 else nc.scalar, wa_rows, wa_scales, r)
+        for r in range(ROWS):
+            load_rows(nc.sync if r == 0 else nc.scalar, x_plane, xt_scales, r)
         load_words(wa_raw, wa_words)
         nc.sync.dma_start(out=x_codes[:].bitcast(I32), in_=xt_words.rearrange("z p c -> p z c").bitcast(I32))
-        for r in range(4):
-            load_rows(nc.scalar, x_plane, xt_scales, r)
+        for r in range(ROWS):
+            load_rows(nc.sync if r < ROWS - 1 else nc.gpsimd, wy_rows, wy_scales, r)
         load_words(wy_raw, wy_words)
-        for r in range(4):
-            load_rows(nc.sync, wy_rows, wy_scales, r)
         nc.sync.dma_start(out=wb_raw[:].bitcast(I32), in_=wb_words[0].bitcast(I32))
-        for r in range(4):
+        for r in range(ROWS):
             load_rows(nc.sync, wb_rows, wb_scales, r)
 
-        deal_plane(nc.vector, wa_plane[0][:], wa_rows[:, 0, :])
-        deal_plane(nc.vector, wa_plane[1][:], wa_rows[:, 1, :])
-        deal_words(wa_codes[0], wa_raw[:, 0, :])
-        deal_words(wa_codes[1], wa_raw[:, 1, :])
-        first_layer(0)
-        first_layer(1)
-        first_layer(2)
-        first_layer(3)
-        deal_plane(nc.gpsimd, wy_plane[0][:], wy_rows[:, 0, :])
-        deal_plane(nc.gpsimd, wy_plane[1][:], wy_rows[:, 1, :])
-        deal_wb(nc.gpsimd)
+        for z in range(PASSES):
+            deal_plane(nc.vector, wa_plane[z][:], wa_rows[:, z, :])
+        for z in range(PASSES):
+            nc.vector.tensor_copy(
+                out=wa_codes[z][:].bitcast(I32).rearrange("p (j b m) -> p b j m", j=PACK, m=LINE),
+                in_=wa_raw[:, z, :].bitcast(I32).rearrange("p (b m j) -> p b j m", j=PACK, m=LINE),
+            )
+        for c in range(CHUNKS):
+            x_product(a_bank[c], wa_codes, wa_plane, c, closes_group=True)
+
+        nc.gpsimd.tensor_copy(
+            out=wb_codes[:].rearrange("p (j m h) -> p j m h", j=PACK, h=2),
+            in_=wb_raw[:].rearrange("p (m j h) -> p j m h", j=PACK, h=2),
+        )
         deal_plane(nc.gpsimd, wb_plane[:], wb_rows[:, 0, :])
-        deal_words(wy_codes[0], wy_raw[:, 0, :])
-        group_sum(0)
-        group_mean(0)
-        deal_words(wy_codes[1], wy_raw[:, 1, :])
-        group_sum(1)
-        group_mean(1)
-        subtract(0)
-        relu_scalar(0)
-        group_sum(2)
-        group_mean(2)
-        skip(0)
-        skip(1)
-        skip(2)
-        subtract(1)
-        relu_scalar(1)
-        quantize_hid(0)
-        second_layer(0)
-        group_sum(3)
-        group_mean(3)
-        skip(3)
-        subtract(2)
-        quantize_hid(1)
-        second_layer(1)
-        store_y(0)
-        relu_vector(2)
-        subtract(3)
-        quantize_hid(2)
-        second_layer(2)
-        store_y(1)
-        relu_vector(3)
-        round_y_vector(0)
-        quantize_hid(3)
-        second_layer(3)
-        store_y(2)
-        round_y_vector(1)
-        quantize_y(0)
-        round_y_vector(2)
-        quantize_y(1)
-        store_y(3)
-        quantize_y(2)
-        round_y_vector(3)
-        quantize_y(3)
-        for q in range(4):
-            queue = nc.sync if q < 2 else nc.scalar
+        nc.vector.tensor_copy(
+            out=wy_plane[:].rearrange("p z (j m) -> p z j m", j=PACK),
+            in_=wy_rows[:].rearrange("p z (m j) -> p z j m", j=PACK),
+        )
+        nc.vector.tensor_copy(
+            out=wy_codes[:].bitcast(I32).rearrange("p z (j b m) -> p z b j m", j=PACK, m=LINE),
+            in_=wy_raw[:].bitcast(I32).rearrange("p z (b m j) -> p z b j m", j=PACK, m=LINE),
+        )
+        wy_pass_codes = [wy_codes[:, z, :] for z in range(PASSES)]
+        wy_pass_plane = [wy_plane[:, z, :] for z in range(PASSES)]
+        for c in range(CHUNKS):
+            x_product(y_bank[c], wy_pass_codes, wy_pass_plane, c, closes_group=False)
+
+        last = CHUNKS - 1
+        for step in range(CHUNKS + 4):
+            if step < CHUNKS:
+                group_mean(step)
+            if 0 <= step - 3 < CHUNKS:
+                second_layer(step - 3)
+            if 0 <= step - 4:
+                store_y(step - 4)
+            if SCALAR_RELU_CHUNKS <= step - 2 < CHUNKS:
+                nc.vector.tensor_scalar_max(out=hid[step - 2][:], in0=diff[step - 2][:], scalar1=0.0)
+            if 0 <= step - 1 < CHUNKS:
+                subtract_mean(step - 1)
+            if 0 <= step - 1 < SCALAR_RELU_CHUNKS:
+                nc.scalar.activation(out=hid[step - 1][:], in_=diff[step - 1][:], func=ACT.Relu)
+            if 0 <= step - 5:
+                round_y(step - 5)
+            if 0 <= step - 6:
+                quantize_y(step - 6)
+
+        quantize_y(last - 1)
+        store_y_codes(slice(0, CHUNK * last))
+        round_y(last)
+        quantize_y(last)
+        store_y_codes(chunk_cols(last))
+        for q in range(ROWS):
+            queue = nc.sync if q < ROWS // 2 else nc.scalar
             queue.dma_start(
-                out=out_2[0, 4 * q : 4 * q + 4, :].bitcast(I32), in_=y_plane[32 * q : 32 * q + 4, :].bitcast(I32)
+                out=out_2[0, ROWS * q : ROWS * (q + 1), :].bitcast(I32),
+                in_=y_plane[QUADRANT * q : QUADRANT * q + ROWS, :].bitcast(I32),
             )

from contextlib import ExitStack

import concourse.mybir as mybir

K, T, R, N = 1024, 512, 512, 512
FLOPS = 2 * K * R * T + 2 * R * N * T + 2 * K * N * T

F32 = mybir.dt.float32
BF16 = mybir.dt.bfloat16
I32 = mybir.dt.int32
U32 = mybir.dt.uint32
U8 = mybir.dt.uint8
FP8X4 = mybir.dt.float8_e4m3fn_x4
FP4X4 = mybir.dt.float4_e2m1fn_x4
ALU = mybir.AluOpType
ACT = mybir.ActivationFunctionType

P = 128
PACK = 4
PASSES = K // (P * PACK)
CHUNK = 128
CHUNKS = T // CHUNK
GROUP = 4
QUADRANT = 32
ROWS = 4
LINE = 4
SCALAR_RELU_CHUNKS = 2


def tile_mix_hidden_less_group_and_skip_pl_kernel(
    tc, xt_words, xt_scales, wa_words, wa_scales, wb_words, wb_scales, wy_words, wy_scales, out_0, out_1, out_2
):
    nc = tc.nc
    with ExitStack() as ctx:
        sb = ctx.enter_context(tc.tile_pool(name="sb", bufs=1))
        ps = ctx.enter_context(tc.psum_pool(name="ps", bufs=1))
        ctx.enter_context(tc.manual_schedule())

        def sbuf_tiles(name, count, shape, dtype):
            return [sb.tile(shape, dtype, name="%s%d" % (name, c), align_bytes=64) for c in range(count)]

        def psum_banks(name):
            return [ps.tile([P, PACK, CHUNK], F32, name="%s%d" % (name, c)) for c in range(CHUNKS)]

        x_codes = sb.tile([P, PASSES, 2 * T], U8, align_bytes=64)
        x_plane = sb.tile([P, PASSES, T], U8, align_bytes=64)
        wa_raw = sb.tile([P, PASSES, R], U32, align_bytes=64)
        wa_codes = sbuf_tiles("wa_codes", PASSES, [P, R], U32)
        wa_rows = sb.tile([P, PASSES, R], U8, align_bytes=64)
        wa_plane = sbuf_tiles("wa_plane", PASSES, [P, R], U8)
        wy_raw = sb.tile([P, PASSES, N], U32, align_bytes=64)
        wy_codes = sb.tile([P, PASSES, N], U32, align_bytes=64)
        wy_rows = sb.tile([P, PASSES, N], U8, align_bytes=64)
        wy_plane = sb.tile([P, PASSES, N], U8, align_bytes=64)
        wb_raw = sb.tile([P, 2 * N], U8, align_bytes=64)
        wb_codes = sb.tile([P, 2 * N], U8, align_bytes=64)
        wb_rows = sb.tile([P, 1, N], U8, align_bytes=64)
        wb_plane = sb.tile([P, N], U8, align_bytes=64)

        a_bank = psum_banks("a_bank")
        y_bank = psum_banks("y_bank")
        sums = sbuf_tiles("sums", CHUNKS, [P, PACK, CHUNK // GROUP], F32)
        means = sbuf_tiles("means", CHUNKS, [P, CHUNK // GROUP, PACK], F32)
        diff = sbuf_tiles("diff", CHUNKS, [P, CHUNK * PACK], BF16)
        hid = sbuf_tiles("hid", CHUNKS, [P, CHUNK * PACK], BF16)
        hid_codes = sbuf_tiles("hid_codes", CHUNKS, [P, CHUNK], U32)
        hid_plane = sbuf_tiles("hid_plane", CHUNKS, [P, CHUNK], U8)
        y_f32 = sbuf_tiles("y_f32", CHUNKS, [P, PACK, CHUNK], F32)
        y_bf16 = sbuf_tiles("y_bf16", CHUNKS, [P, CHUNK * PACK], BF16)
        y_codes = sb.tile([P, T], U32, align_bytes=64)
        y_plane = sb.tile([P, T], U8, align_bytes=64)

        def chunk_cols(c):
            return slice(CHUNK * c, CHUNK * (c + 1))

        def zero(engine, rows):
            engine.memset(rows[:].rearrange("p z c -> p (z c)").bitcast(I32), 0)

        def load_rows(queue, rows, scales, r):
            src = scales.rearrange("z (q r) c -> r q z c", r=ROWS)[r]
            queue.dma_start(out=rows[r:P:QUADRANT, :, :].bitcast(I32), in_=src.bitcast(I32))

        def load_words(raw, words):
            nc.sync.dma_start(out=raw[:].bitcast(I32), in_=words.rearrange("z p n t -> p z (n t)").bitcast(I32))

        def deal_plane(engine, plane, rows):
            engine.tensor_copy(
                out=plane.rearrange("p (j m) -> p j m", j=PACK), in_=rows.rearrange("p (m j) -> p j m", j=PACK)
            )

        def x_product(bank, codes, planes, c, closes_group):
            for z in range(PASSES):
                for j in range(PACK):
                    nc.tensor.matmul_mx(
                        out=bank[:, j, :],
                        lhsT=codes[z][:, P * j : P * (j + 1)].bitcast(FP8X4),
                        lhsT_scale=planes[z][:, P * j : P * (j + 1)],
                        rhs=x_codes[:, z, 2 * CHUNK * c : 2 * CHUNK * (c + 1)].bitcast(FP4X4),
                        rhs_scale=x_plane[:, z, chunk_cols(c)],
                        start=(z == 0 and j == 0),
                        stop=(closes_group and z == PASSES - 1 and j == PACK - 1),
                    )

        def group_mean(c):
            nc.vector.tensor_reduce(
                out=sums[c][:].rearrange("p j b -> p (j b)"),
                in_=a_bank[c][:].rearrange("p j (b g) -> p (j b) g", g=GROUP),
                axis=mybir.AxisListType.X,
                op=ALU.add,
            )
            nc.scalar.activation(
                out=means[c][:], in_=sums[c][:].rearrange("p j b -> p b j"), func=ACT.Copy, scale=1.0 / GROUP
            )

        def subtract_mean(c):
            nc.vector.tensor_tensor(
                out=diff[c][:].rearrange("p (b g j) -> p b g j", g=GROUP, j=PACK),
                in0=a_bank[c][:].rearrange("p j (b g) -> p b g j", g=GROUP),
                in1=means[c][:].unsqueeze(2).to_broadcast([P, CHUNK // GROUP, GROUP, PACK]),
                op=ALU.subtract,
            )

        def second_layer(c):
            nc.vector.quantize_mx(out=hid_codes[c][:].bitcast(FP8X4), scales=hid_plane[c][:], in_=hid[c][:])
            for j in range(PACK):
                nc.tensor.matmul_mx(
                    out=y_bank[c][:, j, :],
                    lhsT=wb_codes[:, 2 * P * j : 2 * P * (j + 1)].bitcast(FP4X4),
                    lhsT_scale=wb_plane[:, P * j : P * (j + 1)],
                    rhs=hid_codes[c][:].bitcast(FP8X4),
                    rhs_scale=hid_plane[c][:],
                    start=False,
                    stop=(j == PACK - 1),
                )

        def store_y(c):
            nc.scalar.copy(out=y_f32[c][:], in_=y_bank[c][:])
            nc.sync.dma_start(out=out_0.rearrange("(p j) t -> p j t", j=PACK)[:, :, chunk_cols(c)], in_=y_f32[c][:])

        def round_y(c):
            nc.vector.tensor_copy(
                out=y_bf16[c][:].rearrange("p (b t j) -> p b j t", j=PACK, t=LINE),
                in_=y_f32[c][:].rearrange("p j (b t) -> p b j t", t=LINE),
            )

        def quantize_y(c):
            cols = chunk_cols(c)
            nc.vector.quantize_mx(out=y_codes[:, cols].bitcast(FP8X4), scales=y_plane[:, cols], in_=y_bf16[c][:])

        def store_y_codes(cols):
            dst = out_1[0].rearrange("p n t -> p (n t)").bitcast(I32)
            nc.sync.dma_start(out=dst[:, cols], in_=y_codes[:, cols].bitcast(I32))

        zero(nc.vector, wa_rows)
        zero(nc.gpsimd, x_plane)
        zero(nc.vector, wy_rows)
        zero(nc.vector, wb_rows)
        for r in range(ROWS):
            load_rows(nc.sync if r < ROWS // 2 else nc.scalar, wa_rows, wa_scales, r)
        for r in range(ROWS):
            load_rows(nc.sync if r == 0 else nc.scalar, x_plane, xt_scales, r)
        load_words(wa_raw, wa_words)
        nc.sync.dma_start(out=x_codes[:].bitcast(I32), in_=xt_words.rearrange("z p c -> p z c").bitcast(I32))
        for r in range(ROWS):
            load_rows(nc.sync if r < ROWS - 1 else nc.gpsimd, wy_rows, wy_scales, r)
        load_words(wy_raw, wy_words)
        nc.sync.dma_start(out=wb_raw[:].bitcast(I32), in_=wb_words[0].bitcast(I32))
        for r in range(ROWS):
            load_rows(nc.sync, wb_rows, wb_scales, r)

        for z in range(PASSES):
            deal_plane(nc.vector, wa_plane[z][:], wa_rows[:, z, :])
        for z in range(PASSES):
            nc.vector.tensor_copy(
                out=wa_codes[z][:].bitcast(I32).rearrange("p (j b m) -> p b j m", j=PACK, m=LINE),
                in_=wa_raw[:, z, :].bitcast(I32).rearrange("p (b m j) -> p b j m", j=PACK, m=LINE),
            )
        for c in range(CHUNKS):
            x_product(a_bank[c], wa_codes, wa_plane, c, closes_group=True)

        nc.gpsimd.tensor_copy(
            out=wb_codes[:].rearrange("p (j m h) -> p j m h", j=PACK, h=2),
            in_=wb_raw[:].rearrange("p (m j h) -> p j m h", j=PACK, h=2),
        )
        deal_plane(nc.gpsimd, wb_plane[:], wb_rows[:, 0, :])
        nc.vector.tensor_copy(
            out=wy_plane[:].rearrange("p z (j m) -> p z j m", j=PACK),
            in_=wy_rows[:].rearrange("p z (m j) -> p z j m", j=PACK),
        )
        nc.vector.tensor_copy(
            out=wy_codes[:].bitcast(I32).rearrange("p z (j b m) -> p z b j m", j=PACK, m=LINE),
            in_=wy_raw[:].bitcast(I32).rearrange("p z (b m j) -> p z b j m", j=PACK, m=LINE),
        )
        wy_pass_codes = [wy_codes[:, z, :] for z in range(PASSES)]
        wy_pass_plane = [wy_plane[:, z, :] for z in range(PASSES)]
        for c in range(CHUNKS):
            x_product(y_bank[c], wy_pass_codes, wy_pass_plane, c, closes_group=False)

        last = CHUNKS - 1
        for step in range(CHUNKS + 4):
            if step < CHUNKS:
                group_mean(step)
            if 0 <= step - 3 < CHUNKS:
                second_layer(step - 3)
            if 0 <= step - 4:
                store_y(step - 4)
            if SCALAR_RELU_CHUNKS <= step - 2 < CHUNKS:
                nc.vector.tensor_scalar_max(out=hid[step - 2][:], in0=diff[step - 2][:], scalar1=0.0)
            if 0 <= step - 1 < CHUNKS:
                subtract_mean(step - 1)
            if 0 <= step - 1 < SCALAR_RELU_CHUNKS:
                nc.scalar.activation(out=hid[step - 1][:], in_=diff[step - 1][:], func=ACT.Relu)
            if 0 <= step - 5:
                round_y(step - 5)
            if 0 <= step - 6:
                quantize_y(step - 6)

        quantize_y(last - 1)
        store_y_codes(slice(0, CHUNK * last))
        round_y(last)
        quantize_y(last)
        store_y_codes(chunk_cols(last))
        for q in range(ROWS):
            queue = nc.sync if q < ROWS // 2 else nc.scalar
            queue.dma_start(
                out=out_2[0, ROWS * q : ROWS * (q + 1), :].bitcast(I32),
                in_=y_plane[QUADRANT * q : QUADRANT * q + ROWS, :].bitcast(I32),
            )
